import numpy as np
import ml_dtypes


def mxq(x, axis, fmt="e4m3"):
    dtype, down = {"e4m3": (ml_dtypes.float8_e4m3fn, 7), "e5m2": (ml_dtypes.float8_e5m2, 14)}[fmt]
    v = np.moveaxis(np.asarray(x, np.float32).astype(ml_dtypes.bfloat16).astype(np.float64), axis, -1)
    blocks = v.reshape(v.shape[:-1] + (-1, 32))
    amax = np.abs(blocks).max(-1, keepdims=True)
    byte = np.maximum(np.where(amax > 0, np.frexp(amax)[1] - 1 + 127, 0) - down, 1)
    scale = np.exp2(byte - 127.0)
    codes = (blocks / scale).astype(np.float32).astype(dtype).astype(np.float64)
    return np.moveaxis((codes * scale).reshape(v.shape), -1, axis)


WIDE = False


def mx_kscale(k):
    if not WIDE:
        return np.ones(k)
    levels = np.array([10, -10, 5, -5, 0])
    if k % 512:
        return np.exp2(np.random.permutation(np.resize(levels, k // 32))).repeat(32)
    a = np.empty((k // 512, 16))
    for p in range(k // 512):
        a[p, :8] = np.random.permutation(np.resize(levels, 8))
        for g in range(8):
            far = levels[np.abs(levels - a[p, g]) >= 10]
            a[p, g + 8] = far[np.random.randint(len(far))]
    return np.exp2(a.ravel()).repeat(32)


def f64(x):
    return np.asarray(x).astype(np.float64)


def striped(idx):
    return np.tile(np.asarray(idx).reshape(-1, 16).T, (8, 1)).astype(np.uint16)


def unstriped(offs):
    return offs[:16].T.reshape(-1).astype(np.int64)


E2M1 = np.array([0.0, 0.5, 1.0, 1.5, 2.0, 3.0, 4.0, 6.0, -0.0, -0.5, -1.0, -1.5, -2.0, -3.0, -4.0, -6.0])


def pack_weight(w, fmt):
    k, n = w.shape
    w = f64(np.asarray(w, np.float32).astype(ml_dtypes.bfloat16)).reshape(k // 32, 32, n)
    amax = np.abs(w).max(1)
    if fmt == "e4m3":
        byte = np.frexp(amax)[1] - 1 + 127 - 7
    else:
        mant, ex = np.frexp(amax / 6.0)
        byte = np.where(mant > 0.5, ex, ex - 1) + 127
    byte = np.clip(np.where(amax > 0, byte, 1), 1, 254)
    scaled = (w * np.exp2(127.0 - byte)[:, None, :]).reshape(k, n).astype(np.float32)
    by_word = np.ascontiguousarray(scaled.reshape(k // 512, 128, 4, n).transpose(0, 1, 3, 2))
    if fmt == "e4m3":
        words = by_word.astype(ml_dtypes.float8_e4m3fn).view(np.uint8)
    else:
        c = by_word.astype(ml_dtypes.float4_e2m1fn).view(np.uint8) & 0xF
        words = (c[..., 0::2] | (c[..., 1::2] << 4)).reshape(k // 512, 128, 2 * n)
    return np.ascontiguousarray(words), np.ascontiguousarray(byte.astype(np.uint8).reshape(k // 512, 16, n))


def unpack_weight(words, scales, fmt):
    g, _, n = scales.shape
    words = np.ascontiguousarray(words).reshape(g, 128, n, -1)
    if fmt == "e4m3":
        vals = words.view(ml_dtypes.float8_e4m3fn).astype(np.float64)
    else:
        nib = np.empty((g, 128, n, 4), np.uint8)
        nib[..., 0::2] = words & 0xF
        nib[..., 1::2] = words >> 4
        vals = E2M1[nib]
    vals = vals * np.repeat(np.exp2(scales.astype(np.float64) - 127.0), 8, axis=1)[..., None]
    return vals.transpose(0, 1, 3, 2).reshape(g * 512, n)


def bf(x):
    return np.asarray(x, np.float32).astype(ml_dtypes.bfloat16)


def planes(Y):
    r, m = Y.shape
    b = f64(bf(Y)).reshape(r // 32, 32, m)
    amax = np.abs(b).max(1)
    byte = np.clip(np.where(amax > 0, np.frexp(amax)[1] - 1 + 127 - 7, 1), 1, 254)
    codes = (b * np.exp2(127.0 - byte)[:, None, :]).reshape(r, m).astype(np.float32).astype(ml_dtypes.float8_e4m3fn).view(np.uint8)
    words = codes.reshape(r // 512, 128, 4, m).transpose(0, 1, 3, 2)
    return np.ascontiguousarray(words), np.ascontiguousarray(byte.astype(np.uint8).reshape(r // 512, 16, m))


D, T, I, Q, E, M = 512, 1024, 512, 512, 512, 1024


def setup_inputs():
    n = np.random.standard_normal
    idx = np.random.permutation(T)[:I]
    idx2 = np.random.permutation(T)[:I]
    idx3 = np.random.permutation(T)[:I]
    idx4 = np.random.permutation(M)[:I]
    fd = mx_kscale(D)
    fq = mx_kscale(Q)
    keysp = pack_weight(n((D, T)) / fd[:, None], "e2m1")
    return {
        "query": (n((D, Q)) * 1.2 / np.sqrt(D) * fd[:, None]).astype(np.float32),
        "keys_words": keysp[0],
        "keys_scales": keysp[1],
        "lam": (np.random.uniform(0.8, 1.8, (Q, 1))).astype(np.float32),
        "qs": (np.random.uniform(0.5, 2.0, (Q, 1)) * fq[:, None]).astype(np.float32),
        "msgs": (n((Q, E)) * 1 / np.sqrt(Q) / fq[:, None]).astype(np.float32),
        "old": (n((E, M)) * 1.0).astype(np.float32),
        "offs": striped(idx),
        "offs2": striped(idx2),
        "offs3": striped(idx3),
        "offs4": striped(idx4),
    }


def reference(query, keys_words, keys_scales, lam, qs, msgs, old, offs, offs2, offs3, offs4):
    idx = unstriped(offs)
    idx2 = unstriped(offs2)
    idx3 = unstriped(offs3)
    idx4 = unstriped(offs4)
    keysu = unpack_weight(keys_words, keys_scales, "e2m1")
    queryq = mxq(f64(query), 0, "e4m3")
    a = queryq.T @ keysu
    lo2 = np.minimum(a[:, idx], a[:, idx2])
    hi2 = np.maximum(a[:, idx], a[:, idx2])
    w = np.maximum(lo2, np.minimum(hi2, a[:, idx3])) * f64(lam)
    wq = w * f64(qs)
    msgsq = mxq(f64(msgs), 0, "e4m3")
    wqq = mxq(wq, 0, "e4m3")
    dl = msgsq.T @ wqq
    df = np.zeros((E, M))
    df[:, idx4] = dl
    y = f64(old) + df
    words, scales = planes(y)
    return y, words, scales

@@ -1,0 +1,277 @@
+from contextlib import ExitStack
+
+import concourse.mybir as mybir
+
+D, T, I, Q, E, M = 512, 1024, 512, 512, 512, 1024
+FLOPS = 2 * D * Q * T + 2 * Q * E * I
+
+F32 = mybir.dt.float32
+BF16 = mybir.dt.bfloat16
+I32 = mybir.dt.int32
+U32 = mybir.dt.uint32
+U16 = mybir.dt.uint16
+U8 = mybir.dt.uint8
+FP8X4 = mybir.dt.float8_e4m3fn_x4
+FP4X4 = mybir.dt.float4_e2m1fn_x4
+ALU = mybir.AluOpType
+COPY = mybir.ActivationFunctionType.Copy
+
+P = 128
+PACK = 4
+BANK = 512
+CHUNK = 256
+CHUNKS = I // CHUNK
+LIST_COLS = CHUNK // 16
+HALF = Q // 2
+QUARTER = M // 4
+VECTOR_GROUPS = 40
+
+
+def tile_attend_middle_deliveredplanes_lean_pl_kernel(
+    tc, query, keys_words, keys_scales, lam, qs, msgs, old, offs, offs2, offs3, offs4, out_0, out_1, out_2
+):
+    nc = tc.nc
+    with ExitStack() as ctx:
+        lists = ctx.enter_context(tc.tile_pool(name="lists", bufs=1))
+        keep = ctx.enter_context(tc.tile_pool(name="keep", bufs=1))
+        work = ctx.enter_context(tc.tile_pool(name="work", bufs=2))
+        psum = ctx.enter_context(tc.psum_pool(name="psum", bufs=8))
+
+        q_rows = query.rearrange("(p j) q -> p j q", j=PACK)
+        q_raw = [keep.tile([P, PACK, HALF], F32, name=f"q_raw{h}") for h in range(2)]
+        for h in range(2):
+            nc.sync.dma_start(out=q_raw[h][:], in_=q_rows[:, :, h * HALF : (h + 1) * HALF])
+        k_words = keep.tile([P, 2 * T], U8, name="k_words", align_bytes=64)
+        nc.sync.dma_start(out=k_words[:].bitcast(I32), in_=keys_words[0].bitcast(I32))
+        k_scales = keep.tile([P, T], U8, name="k_scales", align_bytes=64)
+        for quad in range(4):
+            nc.scalar.dma_start(
+                out=k_scales[32 * quad : 32 * quad + 4, :].bitcast(I32),
+                in_=keys_scales[0, 4 * quad : 4 * quad + 4, :].bitcast(I32),
+            )
+        token_lists = []
+        for n, src in enumerate((offs, offs2, offs3)):
+            t = lists.tile([P, I // 16], U16, name=f"token_list{n}")
+            nc.sync.dma_start(t[:], src)
+            token_lists.append(t)
+        m_raw = keep.tile([P, PACK, E], F32, name="m_raw")
+        nc.sync.dma_start(out=m_raw[:], in_=msgs.rearrange("(p j) e -> p j e", j=PACK))
+        lam_sb = keep.tile([P, PACK], F32, name="lam_sb")
+        nc.sync.dma_start(out=lam_sb[:], in_=lam.rearrange("(p r) o -> p (r o)", r=PACK))
+        qs_sb = keep.tile([P, PACK], F32, name="qs_sb")
+        nc.sync.dma_start(out=qs_sb[:], in_=qs.rearrange("(p r) o -> p (r o)", r=PACK))
+        place_list = lists.tile([P, I // 16], U16, name="place_list")
+        nc.sync.dma_start(place_list[:], offs4)
+        old_rows = old.rearrange("(p j) m -> p j m", j=PACK)
+        old_sb = [keep.tile([P, M], F32, name=f"old_sb{j}") for j in range(PACK)]
+        for j in range(PACK):
+            nc.sync.dma_start(out=old_sb[j][:], in_=old_rows[:, j, :])
+
+        df = [keep.tile([P, M], F32, name=f"df{j}") for j in range(PACK)]
+        for j in range(PACK):
+            (nc.vector if j < 2 else nc.gpsimd).memset(df[j][:], 0.0)
+
+        q_bf = keep.tile([P, PACK, P, PACK], BF16, name="q_bf", align_bytes=64)
+        q_dst = q_bf[:].rearrange("p r s j -> p s j r")
+        groups = HALF // PACK
+
+        def q_src(h):
+            return q_raw[h][:].rearrange("p j (s r) -> p s j r", r=PACK)
+
+        nc.vector.tensor_copy(out=q_dst[:, 0:groups], in_=q_src(0))
+        nc.vector.tensor_copy(out=q_dst[:, groups : groups + VECTOR_GROUPS], in_=q_src(1)[:, 0:VECTOR_GROUPS])
+        nc.scalar.activation(q_dst[:, groups + VECTOR_GROUPS : P], q_src(1)[:, VECTOR_GROUPS:groups], COPY)
+        q_codes = [keep.tile([P, P], U32, name=f"q_codes{r}", align_bytes=64) for r in range(PACK)]
+        q_scales = [keep.tile([P, P], U8, name=f"q_scales{r}", align_bytes=64) for r in range(PACK)]
+        for r in range(PACK):
+            nc.vector.quantize_mx(
+                out=q_codes[r][:].bitcast(FP8X4),
+                scales=q_scales[r][:],
+                in_=q_bf[:, r].rearrange("p s j -> p (s j)"),
+            )
+
+        a = [keep.tile([P, T], F32, name=f"a{r}") for r in range(PACK)]
+        score_banks = {}
+        for r in range(PACK):
+            for h in range(2):
+                bank = psum.tile([P, BANK], F32, name="bank")
+                nc.tensor.matmul_mx(
+                    out=bank[:],
+                    lhsT=q_codes[r][:].bitcast(FP8X4),
+                    lhsT_scale=q_scales[r][:],
+                    rhs=k_words[:, 2 * BANK * h : 2 * BANK * (h + 1)].bitcast(FP4X4),
+                    rhs_scale=k_scales[:, BANK * h : BANK * (h + 1)],
+                    start=True,
+                    stop=True,
+                )
+                score_banks[r, h] = bank
+
+        def empty_scores(r):
+            nc.vector.tensor_copy(out=a[r][:, 0:BANK], in_=score_banks[r, 0][:])
+            nc.scalar.activation(a[r][:, BANK:T], score_banks[r, 1][:], COPY)
+
+        picked = {}
+
+        def gather(n, r, c, on_vector):
+            g = keep.tile([P, CHUNK], F32, name=f"picked{n}_{r}_{c}")
+            src = a[r][:].indirect(token_lists[n][:, c * LIST_COLS : (c + 1) * LIST_COLS])
+            if on_vector:
+                nc.vector.tensor_copy(g[:], src)
+            else:
+                nc.scalar.activation(g[:], src, COPY)
+            picked[n, r, c] = g
+
+        w_rows = [keep.tile([P, PACK, CHUNK], BF16, name=f"w_rows{c}") for c in range(CHUNKS)]
+
+        def weigh(r, c):
+            g0, g1, g2 = (picked[n, r, c] for n in range(3))
+            hi = work.tile([P, CHUNK], F32, name="hi")
+            lo = work.tile([P, CHUNK], F32, name="lo")
+            cut = work.tile([P, CHUNK], F32, name="cut")
+            mid = work.tile([P, CHUNK], F32, name="mid")
+            nc.vector.tensor_tensor(hi[:], g0[:], g1[:], ALU.max)
+            nc.vector.tensor_tensor(lo[:], g0[:], g1[:], ALU.min)
+            nc.vector.tensor_tensor(cut[:], hi[:], g2[:], ALU.min)
+            nc.vector.tensor_tensor(mid[:], lo[:], cut[:], ALU.max)
+            nc.vector.tensor_scalar(
+                w_rows[c][:, r, :], mid[:], lam_sb[:, r : r + 1], qs_sb[:, r : r + 1], ALU.mult, ALU.mult
+            )
+
+        m_codes = keep.tile([P, E], U32, name="m_codes", align_bytes=64)
+        m_scales = keep.tile([P, E], U8, name="m_scales", align_bytes=64)
+        m_bf = keep.tile([P, PACK, P, PACK], BF16, name="m_bf", align_bytes=64)
+
+        def deal_msgs():
+            nc.vector.tensor_copy(
+                out=m_bf[:].rearrange("p t s j -> p s j t"), in_=m_raw[:].rearrange("p j (s t) -> p s j t", t=PACK)
+            )
+
+        def quantise_msgs():
+            nc.vector.quantize_mx(
+                out=m_codes[:].bitcast(FP8X4), scales=m_scales[:], in_=m_bf[:].rearrange("p t s j -> p (t s j)")
+            )
+
+        dl_banks = {}
+
+        def multiply(c):
+            w_bf = keep.tile([P, CHUNK, PACK], BF16, name=f"w_bf{c}", align_bytes=64)
+            nc.vector.tensor_copy(
+                out=w_bf[:].rearrange("p (b i) r -> p b r i", i=4), in_=w_rows[c][:].rearrange("p r (b i) -> p b r i", i=4)
+            )
+            w_codes = keep.tile([P, CHUNK], U32, name=f"w_codes{c}", align_bytes=64)
+            w_scales = keep.tile([P, CHUNK], U8, name=f"w_scales{c}", align_bytes=64)
+            nc.vector.quantize_mx(
+                out=w_codes[:].bitcast(FP8X4), scales=w_scales[:], in_=w_bf[:].rearrange("p i r -> p (i r)")
+            )
+            for pair in range(2):
+                bank = psum.tile([P, BANK], F32, name="bank")
+                for u in range(2):
+                    j = 2 * pair + u
+                    nc.tensor.matmul_mx(
+                        out=bank[:, u * CHUNK : (u + 1) * CHUNK],
+                        lhsT=m_codes[:, j * P : (j + 1) * P].bitcast(FP8X4),
+                        lhsT_scale=m_scales[:, j * P : (j + 1) * P],
+                        rhs=w_codes[:].bitcast(FP8X4),
+                        rhs_scale=w_scales[:],
+                        start=True,
+                        stop=True,
+                    )
+                dl_banks[c, pair] = bank
+
+        dl = {}
+
+        def empty_sums(c, pair, on_vector):
+            t = keep.tile([P, BANK], F32, name=f"dl{c}_{pair}")
+            if on_vector:
+                nc.vector.tensor_copy(out=t[:], in_=dl_banks[c, pair][:])
+            else:
+                nc.scalar.activation(t[:], dl_banks[c, pair][:], COPY)
+            dl[c, pair] = t
+
+        def scatter(j, c, on_vector):
+            src = dl[c, j // 2][:, (j % 2) * CHUNK : (j % 2 + 1) * CHUNK]
+            dst = df[j][:].indirect(place_list[:, c * LIST_COLS : (c + 1) * LIST_COLS])
+            if on_vector:
+                nc.vector.tensor_copy(dst, src)
+            else:
+                nc.scalar.activation(dst, src, COPY)
+
+        y = keep.tile([P, PACK, M], F32, name="y")
+        out_rows = out_0.rearrange("(p j) m -> p j m", j=PACK)
+
+        def add_old(j, cols):
+            nc.vector.tensor_tensor(y[:, j, cols], old_sb[j][:, cols], df[j][:, cols], ALU.add)
+
+        def store_rows(j):
+            nc.sync.dma_start(out=out_rows[:, j, :], in_=y[:, j, :])
+
+        y_codes = keep.tile([P, M], U32, name="y_codes", align_bytes=64)
+        y_scales = keep.tile([P, M], U8, name="y_scales", align_bytes=64)
+        y_bf = [keep.tile([P, QUARTER, PACK], BF16, name=f"y_bf{k}", align_bytes=64) for k in range(4)]
+
+        def weave(k, on_vector):
+            cols = slice(k * QUARTER, (k + 1) * QUARTER)
+            dst = y_bf[k][:].rearrange("p (b i) j -> p b j i", i=4)
+            src = y[:, :, cols].rearrange("p j (b i) -> p b j i", i=4)
+            if on_vector:
+                nc.vector.tensor_copy(out=dst, in_=src)
+            else:
+                nc.scalar.activation(dst, src, COPY)
+
+        def quantise_y(k):
+            cols = slice(k * QUARTER, (k + 1) * QUARTER)
+            nc.vector.quantize_mx(
+                out=y_codes[:, cols].bitcast(FP8X4), scales=y_scales[:, cols], in_=y_bf[k][:].rearrange("p m j -> p (m j)")
+            )
+
+        for r in range(PACK):
+            empty_scores(r)
+            gather(0, r, 0, True)
+            gather(1, r, 0, False)
+            gather(2, r, 0, False)
+            if r == 1:
+                deal_msgs()
+            if r > 0:
+                weigh(r - 1, 0)
+        quantise_msgs()
+        weigh(PACK - 1, 0)
+        for r in range(PACK):
+            for n in range(3):
+                gather(n, r, 1, False)
+        multiply(0)
+        for r in range(PACK):
+            weigh(r, 1)
+        for pair in range(2):
+            empty_sums(0, pair, False)
+            scatter(2 * pair, 0, False)
+            scatter(2 * pair + 1, 0, False)
+        multiply(1)
+        empty_sums(1, 0, True)
+        scatter(0, 1, True)
+        scatter(1, 1, True)
+        empty_sums(1, 1, False)
+        scatter(2, 1, False)
+        scatter(3, 1, False)
+        whole = slice(0, M)
+        for j in range(3):
+            add_old(j, whole)
+            store_rows(j)
+        for k in range(4):
+            add_old(3, slice(k * QUARTER, (k + 1) * QUARTER))
+        store_rows(3)
+        weave(0, False)
+        weave(1, True)
+        weave(2, False)
+        weave(3, True)
+        words_out = out_1[0].rearrange("p m t -> p (m t)").bitcast(I32)
+        for k in (1, 0, 3, 2):
+            quantise_y(k)
+            if k in (0, 2):
+                cols = slice(k * QUARTER, (k + 2) * QUARTER)
+                nc.sync.dma_start(out=words_out[:, cols], in_=y_codes[:, cols].bitcast(I32))
+        for quad in range(4):
+            eng = nc.scalar if quad % 2 else nc.sync
+            eng.dma_start(
+                out=out_2[0, 4 * quad : 4 * quad + 4, :].bitcast(I32),
+                in_=y_scales[32 * quad : 32 * quad + 4, :].bitcast(I32),
+            )

@@ -24,6 +24,7 @@ CHUNKS = I // CHUNK
 LIST_COLS = CHUNK // 16
 HALF = Q // 2
 QUARTER = M // 4
+PART = CHUNK // 2
 VECTOR_GROUPS = 40
 
 
@@ -121,21 +122,20 @@ def tile_attend_middle_deliveredplanes_lean_pl_kernel(
                 nc.scalar.activation(g[:], src, COPY)
             picked[n, r, c] = g
 
-        w_rows = [keep.tile([P, PACK, CHUNK], BF16, name=f"w_rows{c}") for c in range(CHUNKS)]
+        factor = keep.tile([P, PACK], F32, name="factor")
+        nc.vector.tensor_tensor(factor[:], lam_sb[:], qs_sb[:], ALU.mult)
+        lo = [keep.tile([P, PACK, CHUNK], F32, name=f"lo{c}") for c in range(CHUNKS)]
+        cut = [keep.tile([P, PACK, CHUNK], F32, name=f"cut{c}") for c in range(CHUNKS)]
 
         def weigh(r, c):
             g0, g1, g2 = (picked[n, r, c] for n in range(3))
+            f = factor[:, r : r + 1]
+            first = work.tile([P, CHUNK], F32, name="first")
             hi = work.tile([P, CHUNK], F32, name="hi")
-            lo = work.tile([P, CHUNK], F32, name="lo")
-            cut = work.tile([P, CHUNK], F32, name="cut")
-            mid = work.tile([P, CHUNK], F32, name="mid")
-            nc.vector.tensor_tensor(hi[:], g0[:], g1[:], ALU.max)
-            nc.vector.tensor_tensor(lo[:], g0[:], g1[:], ALU.min)
-            nc.vector.tensor_tensor(cut[:], hi[:], g2[:], ALU.min)
-            nc.vector.tensor_tensor(mid[:], lo[:], cut[:], ALU.max)
-            nc.vector.tensor_scalar(
-                w_rows[c][:, r, :], mid[:], lam_sb[:, r : r + 1], qs_sb[:, r : r + 1], ALU.mult, ALU.mult
-            )
+            nc.vector.tensor_scalar(first[:], g0[:], f, None, ALU.mult)
+            nc.vector.scalar_tensor_tensor(hi[:], g1[:], f, first[:], ALU.mult, ALU.max)
+            nc.vector.scalar_tensor_tensor(lo[c][:, r, :], g1[:], f, first[:], ALU.mult, ALU.min)
+            nc.vector.scalar_tensor_tensor(cut[c][:, r, :], g2[:], f, hi[:], ALU.mult, ALU.min)
 
         m_codes = keep.tile([P, E], U32, name="m_codes", align_bytes=64)
         m_scales = keep.tile([P, E], U8, name="m_scales", align_bytes=64)
@@ -154,43 +154,51 @@ def tile_attend_middle_deliveredplanes_lean_pl_kernel(
         dl_banks = {}
 
         def multiply(c):
-            w_bf = keep.tile([P, CHUNK, PACK], BF16, name=f"w_bf{c}", align_bytes=64)
-            nc.vector.tensor_copy(
-                out=w_bf[:].rearrange("p (b i) r -> p b r i", i=4), in_=w_rows[c][:].rearrange("p r (b i) -> p b r i", i=4)
-            )
-            w_codes = keep.tile([P, CHUNK], U32, name=f"w_codes{c}", align_bytes=64)
-            w_scales = keep.tile([P, CHUNK], U8, name=f"w_scales{c}", align_bytes=64)
-            nc.vector.quantize_mx(
-                out=w_codes[:].bitcast(FP8X4), scales=w_scales[:], in_=w_bf[:].rearrange("p i r -> p (i r)")
-            )
-            for pair in range(2):
-                bank = psum.tile([P, BANK], F32, name="bank")
-                for u in range(2):
-                    j = 2 * pair + u
-                    nc.tensor.matmul_mx(
-                        out=bank[:, u * CHUNK : (u + 1) * CHUNK],
-                        lhsT=m_codes[:, j * P : (j + 1) * P].bitcast(FP8X4),
-                        lhsT_scale=m_scales[:, j * P : (j + 1) * P],
-                        rhs=w_codes[:].bitcast(FP8X4),
-                        rhs_scale=w_scales[:],
-                        start=True,
-                        stop=True,
-                    )
-                dl_banks[c, pair] = bank
+            parts = []
+            for h in range(2):
+                cols = slice(h * PART, (h + 1) * PART)
+                w_bf = keep.tile([P, PART, PACK], BF16, name=f"w_bf{c}_{h}", align_bytes=64)
+                nc.vector.tensor_tensor(
+                    w_bf[:].rearrange("p (b i) r -> p b r i", i=4),
+                    lo[c][:, :, cols].rearrange("p r (b i) -> p b r i", i=4),
+                    cut[c][:, :, cols].rearrange("p r (b i) -> p b r i", i=4),
+                    ALU.max,
+                )
+                parts.append(w_bf)
+            for h in range(2):
+                w_codes = keep.tile([P, PART], U32, name=f"w_codes{c}_{h}", align_bytes=64)
+                w_scales = keep.tile([P, PART], U8, name=f"w_scales{c}_{h}", align_bytes=64)
+                nc.vector.quantize_mx(
+                    out=w_codes[:].bitcast(FP8X4), scales=w_scales[:], in_=parts[h][:].rearrange("p i r -> p (i r)")
+                )
+                for pair in range(2):
+                    bank = psum.tile([P, 2, PART], F32, name="bank")
+                    for u in range(2):
+                        j = 2 * pair + u
+                        nc.tensor.matmul_mx(
+                            out=bank[:, u, :],
+                            lhsT=m_codes[:, j * P : (j + 1) * P].bitcast(FP8X4),
+                            lhsT_scale=m_scales[:, j * P : (j + 1) * P],
+                            rhs=w_codes[:].bitcast(FP8X4),
+                            rhs_scale=w_scales[:],
+                            start=True,
+                            stop=True,
+                        )
+                    dl_banks[c, h, pair] = bank
 
-        dl = {}
+        dl = {(c, pair): keep.tile([P, 2, CHUNK], F32, name=f"dl{c}_{pair}") for c in range(CHUNKS) for pair in range(2)}
 
-        def empty_sums(c, pair, on_vector):
-            t = keep.tile([P, BANK], F32, name=f"dl{c}_{pair}")
+        def empty_sums(c, h, pair, on_vector):
+            dst = dl[c, pair][:, :, h * PART : (h + 1) * PART]
             if on_vector:
-                nc.vector.tensor_copy(out=t[:], in_=dl_banks[c, pair][:])
+                nc.vector.tensor_copy(out=dst, in_=dl_banks[c, h, pair][:])
             else:
-                nc.scalar.activation(t[:], dl_banks[c, pair][:], COPY)
-            dl[c, pair] = t
+                nc.scalar.activation(dst, dl_banks[c, h, pair][:], COPY)
 
-        def scatter(j, c, on_vector):
-            src = dl[c, j // 2][:, (j % 2) * CHUNK : (j % 2 + 1) * CHUNK]
-            dst = df[j][:].indirect(place_list[:, c * LIST_COLS : (c + 1) * LIST_COLS])
+        def scatter(j, c, h0, h1, on_vector):
+            src = dl[c, j // 2][:, j % 2, h0 * PART : h1 * PART]
+            first_col = c * LIST_COLS
+            dst = df[j][:].indirect(place_list[:, first_col + h0 * PART // 16 : first_col + h1 * PART // 16])
             if on_vector:
                 nc.vector.tensor_copy(dst, src)
             else:
@@ -227,7 +235,7 @@ def tile_attend_middle_deliveredplanes_lean_pl_kernel(
         for r in range(PACK):
             empty_scores(r)
             gather(0, r, 0, True)
-            gather(1, r, 0, False)
+            gather(1, r, 0, r == 0)
             gather(2, r, 0, False)
             if r == 1:
                 deal_msgs()
@@ -242,16 +250,20 @@ def tile_attend_middle_deliveredplanes_lean_pl_kernel(
         for r in range(PACK):
             weigh(r, 1)
         for pair in range(2):
-            empty_sums(0, pair, False)
-            scatter(2 * pair, 0, False)
-            scatter(2 * pair + 1, 0, False)
+            empty_sums(0, 0, pair, False)
+            empty_sums(0, 1, pair, False)
+            scatter(2 * pair, 0, 0, 2, False)
+            scatter(2 * pair + 1, 0, 0, 2, False)
         multiply(1)
-        empty_sums(1, 0, True)
-        scatter(0, 1, True)
-        scatter(1, 1, True)
-        empty_sums(1, 1, False)
-        scatter(2, 1, False)
-        scatter(3, 1, False)
+        empty_sums(1, 0, 0, True)
+        scatter(0, 1, 0, 1, True)
+        empty_sums(1, 1, 0, True)
+        scatter(0, 1, 1, 2, True)
+        scatter(1, 1, 0, 2, True)
+        empty_sums(1, 0, 1, False)
+        empty_sums(1, 1, 1, False)
+        scatter(2, 1, 0, 2, False)
+        scatter(3, 1, 0, 2, False)
         whole = slice(0, M)
         for j in range(3):
             add_old(j, whole)
@@ -266,9 +278,8 @@ def tile_attend_middle_deliveredplanes_lean_pl_kernel(
         words_out = out_1[0].rearrange("p m t -> p (m t)").bitcast(I32)
         for k in (1, 0, 3, 2):
             quantise_y(k)
-            if k in (0, 2):
-                cols = slice(k * QUARTER, (k + 2) * QUARTER)
-                nc.sync.dma_start(out=words_out[:, cols], in_=y_codes[:, cols].bitcast(I32))
+            cols = slice(k * QUARTER, (k + 1) * QUARTER)
+            nc.sync.dma_start(out=words_out[:, cols], in_=y_codes[:, cols].bitcast(I32))
         for quad in range(4):
             eng = nc.scalar if quad % 2 else nc.sync
             eng.dma_start(

@@ -58,9 +58,9 @@ def tile_attend_middle_deliveredplanes_lean_pl_kernel(
         m_raw = keep.tile([P, PACK, E], F32, name="m_raw")
         nc.sync.dma_start(out=m_raw[:], in_=msgs.rearrange("(p j) e -> p j e", j=PACK))
         lam_sb = keep.tile([P, PACK], F32, name="lam_sb")
-        nc.sync.dma_start(out=lam_sb[:], in_=lam.rearrange("(p r) o -> p (r o)", r=PACK))
+        nc.gpsimd.dma_start(out=lam_sb[:], in_=lam.rearrange("(p r) o -> p (r o)", r=PACK))
         qs_sb = keep.tile([P, PACK], F32, name="qs_sb")
-        nc.sync.dma_start(out=qs_sb[:], in_=qs.rearrange("(p r) o -> p (r o)", r=PACK))
+        nc.gpsimd.dma_start(out=qs_sb[:], in_=qs.rearrange("(p r) o -> p (r o)", r=PACK))
         place_list = lists.tile([P, I // 16], U16, name="place_list")
         nc.sync.dma_start(place_list[:], offs4)
         old_rows = old.rearrange("(p j) m -> p j m", j=PACK)
@@ -70,7 +70,7 @@ def tile_attend_middle_deliveredplanes_lean_pl_kernel(
 
         df = [keep.tile([P, M], F32, name=f"df{j}") for j in range(PACK)]
         for j in range(PACK):
-            (nc.vector if j < 2 else nc.gpsimd).memset(df[j][:], 0.0)
+            (nc.vector if j < 3 else nc.gpsimd).memset(df[j][:], 0.0)
 
         q_bf = keep.tile([P, PACK, P, PACK], BF16, name="q_bf", align_bytes=64)
         q_dst = q_bf[:].rearrange("p r s j -> p s j r")
@@ -108,33 +108,38 @@ def tile_attend_middle_deliveredplanes_lean_pl_kernel(
                 score_banks[r, h] = bank
 
         def empty_scores(r):
-            nc.vector.tensor_copy(out=a[r][:, 0:BANK], in_=score_banks[r, 0][:])
+            if r < 2:
+                nc.vector.tensor_copy(out=a[r][:, 0:BANK], in_=score_banks[r, 0][:])
+            else:
+                nc.scalar.activation(a[r][:, 0:BANK], score_banks[r, 0][:], COPY)
             nc.scalar.activation(a[r][:, BANK:T], score_banks[r, 1][:], COPY)
+
+        factor_rows = keep.tile([P, PACK, CHUNK], F32, name="q_raw1")
+        for r in range(PACK):
+            nc.scalar.activation(
+                factor_rows[:, r, :], lam_sb[:, r : r + 1].to_broadcast([P, CHUNK]), COPY, scale=qs_sb[:, r : r + 1]
+            )
 
         picked = {}
 
-        def gather(n, r, c, on_vector):
+        def gather(n, r, c):
             g = keep.tile([P, CHUNK], F32, name=f"picked{n}_{r}_{c}")
             src = a[r][:].indirect(token_lists[n][:, c * LIST_COLS : (c + 1) * LIST_COLS])
-            if on_vector:
-                nc.vector.tensor_copy(g[:], src)
+            if n == 0:
+                nc.vector.tensor_tensor(g[:], src, factor_rows[:, r, :], ALU.mult)
             else:
                 nc.scalar.activation(g[:], src, COPY)
             picked[n, r, c] = g
 
-        factor = keep.tile([P, PACK], F32, name="factor")
-        nc.vector.tensor_tensor(factor[:], lam_sb[:], qs_sb[:], ALU.mult)
         lo = [keep.tile([P, PACK, CHUNK], F32, name=f"lo{c}") for c in range(CHUNKS)]
         cut = [keep.tile([P, PACK, CHUNK], F32, name=f"cut{c}") for c in range(CHUNKS)]
 
         def weigh(r, c):
             g0, g1, g2 = (picked[n, r, c] for n in range(3))
-            f = factor[:, r : r + 1]
-            first = work.tile([P, CHUNK], F32, name="first")
+            f = factor_rows[:, r, 0:1]
             hi = work.tile([P, CHUNK], F32, name="hi")
-            nc.vector.tensor_scalar(first[:], g0[:], f, None, ALU.mult)
-            nc.vector.scalar_tensor_tensor(hi[:], g1[:], f, first[:], ALU.mult, ALU.max)
-            nc.vector.scalar_tensor_tensor(lo[c][:, r, :], g1[:], f, first[:], ALU.mult, ALU.min)
+            nc.vector.scalar_tensor_tensor(hi[:], g1[:], f, g0[:], ALU.mult, ALU.max)
+            nc.vector.scalar_tensor_tensor(lo[c][:, r, :], g1[:], f, g0[:], ALU.mult, ALU.min)
             nc.vector.scalar_tensor_tensor(cut[c][:, r, :], g2[:], f, hi[:], ALU.mult, ALU.min)
 
         m_codes = keep.tile([P, E], U32, name="m_codes", align_bytes=64)
@@ -234,9 +239,8 @@ def tile_attend_middle_deliveredplanes_lean_pl_kernel(
 
         for r in range(PACK):
             empty_scores(r)
-            gather(0, r, 0, True)
-            gather(1, r, 0, r == 0)
-            gather(2, r, 0, False)
+            for n in range(3):
+                gather(n, r, 0)
             if r == 1:
                 deal_msgs()
             if r > 0:
@@ -244,10 +248,13 @@ def tile_attend_middle_deliveredplanes_lean_pl_kernel(
         quantise_msgs()
         weigh(PACK - 1, 0)
         for r in range(PACK):
-            for n in range(3):
-                gather(n, r, 1, False)
+            gather(1, r, 1)
+            gather(2, r, 1)
+        gather(0, 0, 1)
         multiply(0)
         for r in range(PACK):
+            if r + 1 < PACK:
+                gather(0, r + 1, 1)
             weigh(r, 1)
         for pair in range(2):
             empty_sums(0, 0, pair, False)
@@ -259,7 +266,8 @@ def tile_attend_middle_deliveredplanes_lean_pl_kernel(
         scatter(0, 1, 0, 1, True)
         empty_sums(1, 1, 0, True)
         scatter(0, 1, 1, 2, True)
-        scatter(1, 1, 0, 2, True)
+        scatter(1, 1, 0, 1, True)
+        scatter(1, 1, 1, 2, False)
         empty_sums(1, 0, 1, False)
         empty_sums(1, 1, 1, False)
         scatter(2, 1, 0, 2, False)

from contextlib import ExitStack

import concourse.mybir as mybir

D, T, I, Q, E, M = 512, 1024, 512, 512, 512, 1024
FLOPS = 2 * D * Q * T + 2 * Q * E * I

F32 = mybir.dt.float32
BF16 = mybir.dt.bfloat16
I32 = mybir.dt.int32
U32 = mybir.dt.uint32
U16 = mybir.dt.uint16
U8 = mybir.dt.uint8
FP8X4 = mybir.dt.float8_e4m3fn_x4
FP4X4 = mybir.dt.float4_e2m1fn_x4
ALU = mybir.AluOpType
COPY = mybir.ActivationFunctionType.Copy

P = 128
PACK = 4
BANK = 512
CHUNK = 256
CHUNKS = I // CHUNK
LIST_COLS = CHUNK // 16
HALF = Q // 2
QUARTER = M // 4
PART = CHUNK // 2
VECTOR_GROUPS = 40


def tile_attend_middle_deliveredplanes_lean_pl_kernel(
    tc, query, keys_words, keys_scales, lam, qs, msgs, old, offs, offs2, offs3, offs4, out_0, out_1, out_2
):
    nc = tc.nc
    with ExitStack() as ctx:
        lists = ctx.enter_context(tc.tile_pool(name="lists", bufs=1))
        keep = ctx.enter_context(tc.tile_pool(name="keep", bufs=1))
        work = ctx.enter_context(tc.tile_pool(name="work", bufs=2))
        psum = ctx.enter_context(tc.psum_pool(name="psum", bufs=8))

        q_rows = query.rearrange("(p j) q -> p j q", j=PACK)
        q_raw = [keep.tile([P, PACK, HALF], F32, name=f"q_raw{h}") for h in range(2)]
        for h in range(2):
            nc.sync.dma_start(out=q_raw[h][:], in_=q_rows[:, :, h * HALF : (h + 1) * HALF])
        k_words = keep.tile([P, 2 * T], U8, name="k_words", align_bytes=64)
        nc.sync.dma_start(out=k_words[:].bitcast(I32), in_=keys_words[0].bitcast(I32))
        k_scales = keep.tile([P, T], U8, name="k_scales", align_bytes=64)
        for quad in range(4):
            nc.scalar.dma_start(
                out=k_scales[32 * quad : 32 * quad + 4, :].bitcast(I32),
                in_=keys_scales[0, 4 * quad : 4 * quad + 4, :].bitcast(I32),
            )
        token_lists = []
        for n, src in enumerate((offs, offs2, offs3)):
            t = lists.tile([P, I // 16], U16, name=f"token_list{n}")
            nc.sync.dma_start(t[:], src)
            token_lists.append(t)
        m_raw = keep.tile([P, PACK, E], F32, name="m_raw")
        nc.sync.dma_start(out=m_raw[:], in_=msgs.rearrange("(p j) e -> p j e", j=PACK))
        lam_sb = keep.tile([P, PACK], F32, name="lam_sb")
        nc.gpsimd.dma_start(out=lam_sb[:], in_=lam.rearrange("(p r) o -> p (r o)", r=PACK))
        qs_sb = keep.tile([P, PACK], F32, name="qs_sb")
        nc.gpsimd.dma_start(out=qs_sb[:], in_=qs.rearrange("(p r) o -> p (r o)", r=PACK))
        place_list = lists.tile([P, I // 16], U16, name="place_list")
        nc.sync.dma_start(place_list[:], offs4)
        old_rows = old.rearrange("(p j) m -> p j m", j=PACK)
        old_sb = [keep.tile([P, M], F32, name=f"old_sb{j}") for j in range(PACK)]
        for j in range(PACK):
            nc.sync.dma_start(out=old_sb[j][:], in_=old_rows[:, j, :])

        df = [keep.tile([P, M], F32, name=f"df{j}") for j in range(PACK)]
        for j in range(PACK):
            (nc.vector if j < 3 else nc.gpsimd).memset(df[j][:], 0.0)

        q_bf = keep.tile([P, PACK, P, PACK], BF16, name="q_bf", align_bytes=64)
        q_dst = q_bf[:].rearrange("p r s j -> p s j r")
        groups = HALF // PACK

        def q_src(h):
            return q_raw[h][:].rearrange("p j (s r) -> p s j r", r=PACK)

        nc.vector.tensor_copy(out=q_dst[:, 0:groups], in_=q_src(0))
        nc.vector.tensor_copy(out=q_dst[:, groups : groups + VECTOR_GROUPS], in_=q_src(1)[:, 0:VECTOR_GROUPS])
        nc.scalar.activation(q_dst[:, groups + VECTOR_GROUPS : P], q_src(1)[:, VECTOR_GROUPS:groups], COPY)
        q_codes = [keep.tile([P, P], U32, name=f"q_codes{r}", align_bytes=64) for r in range(PACK)]
        q_scales = [keep.tile([P, P], U8, name=f"q_scales{r}", align_bytes=64) for r in range(PACK)]
        for r in range(PACK):
            nc.vector.quantize_mx(
                out=q_codes[r][:].bitcast(FP8X4),
                scales=q_scales[r][:],
                in_=q_bf[:, r].rearrange("p s j -> p (s j)"),
            )

        a = [keep.tile([P, T], F32, name=f"a{r}") for r in range(PACK)]
        score_banks = {}
        for r in range(PACK):
            for h in range(2):
                bank = psum.tile([P, BANK], F32, name="bank")
                nc.tensor.matmul_mx(
                    out=bank[:],
                    lhsT=q_codes[r][:].bitcast(FP8X4),
                    lhsT_scale=q_scales[r][:],
                    rhs=k_words[:, 2 * BANK * h : 2 * BANK * (h + 1)].bitcast(FP4X4),
                    rhs_scale=k_scales[:, BANK * h : BANK * (h + 1)],
                    start=True,
                    stop=True,
                )
                score_banks[r, h] = bank

        def empty_scores(r):
            if r < 2:
                nc.vector.tensor_copy(out=a[r][:, 0:BANK], in_=score_banks[r, 0][:])
            else:
                nc.scalar.activation(a[r][:, 0:BANK], score_banks[r, 0][:], COPY)
            nc.scalar.activation(a[r][:, BANK:T], score_banks[r, 1][:], COPY)

        factor_rows = keep.tile([P, PACK, CHUNK], F32, name="q_raw1")
        for r in range(PACK):
            nc.scalar.activation(
                factor_rows[:, r, :], lam_sb[:, r : r + 1].to_broadcast([P, CHUNK]), COPY, scale=qs_sb[:, r : r + 1]
            )

        picked = {}

        def gather(n, r, c):
            g = keep.tile([P, CHUNK], F32, name=f"picked{n}_{r}_{c}")
            src = a[r][:].indirect(token_lists[n][:, c * LIST_COLS : (c + 1) * LIST_COLS])
            if n == 0:
                nc.vector.tensor_tensor(g[:], src, factor_rows[:, r, :], ALU.mult)
            else:
                nc.scalar.activation(g[:], src, COPY)
            picked[n, r, c] = g

        lo = [keep.tile([P, PACK, CHUNK], F32, name=f"lo{c}") for c in range(CHUNKS)]
        cut = [keep.tile([P, PACK, CHUNK], F32, name=f"cut{c}") for c in range(CHUNKS)]

        def weigh(r, c):
            g0, g1, g2 = (picked[n, r, c] for n in range(3))
            f = factor_rows[:, r, 0:1]
            hi = work.tile([P, CHUNK], F32, name="hi")
            nc.vector.scalar_tensor_tensor(hi[:], g1[:], f, g0[:], ALU.mult, ALU.max)
            nc.vector.scalar_tensor_tensor(lo[c][:, r, :], g1[:], f, g0[:], ALU.mult, ALU.min)
            nc.vector.scalar_tensor_tensor(cut[c][:, r, :], g2[:], f, hi[:], ALU.mult, ALU.min)

        m_codes = keep.tile([P, E], U32, name="m_codes", align_bytes=64)
        m_scales = keep.tile([P, E], U8, name="m_scales", align_bytes=64)
        m_bf = keep.tile([P, PACK, P, PACK], BF16, name="m_bf", align_bytes=64)

        def deal_msgs():
            nc.vector.tensor_copy(
                out=m_bf[:].rearrange("p t s j -> p s j t"), in_=m_raw[:].rearrange("p j (s t) -> p s j t", t=PACK)
            )

        def quantise_msgs():
            nc.vector.quantize_mx(
                out=m_codes[:].bitcast(FP8X4), scales=m_scales[:], in_=m_bf[:].rearrange("p t s j -> p (t s j)")
            )

        dl_banks = {}

        def multiply(c):
            parts = []
            for h in range(2):
                cols = slice(h * PART, (h + 1) * PART)
                w_bf = keep.tile([P, PART, PACK], BF16, name=f"w_bf{c}_{h}", align_bytes=64)
                nc.vector.tensor_tensor(
                    w_bf[:].rearrange("p (b i) r -> p b r i", i=4),
                    lo[c][:, :, cols].rearrange("p r (b i) -> p b r i", i=4),
                    cut[c][:, :, cols].rearrange("p r (b i) -> p b r i", i=4),
                    ALU.max,
                )
                parts.append(w_bf)
            for h in range(2):
                w_codes = keep.tile([P, PART], U32, name=f"w_codes{c}_{h}", align_bytes=64)
                w_scales = keep.tile([P, PART], U8, name=f"w_scales{c}_{h}", align_bytes=64)
                nc.vector.quantize_mx(
                    out=w_codes[:].bitcast(FP8X4), scales=w_scales[:], in_=parts[h][:].rearrange("p i r -> p (i r)")
                )
                for pair in range(2):
                    bank = psum.tile([P, 2, PART], F32, name="bank")
                    for u in range(2):
                        j = 2 * pair + u
                        nc.tensor.matmul_mx(
                            out=bank[:, u, :],
                            lhsT=m_codes[:, j * P : (j + 1) * P].bitcast(FP8X4),
                            lhsT_scale=m_scales[:, j * P : (j + 1) * P],
                            rhs=w_codes[:].bitcast(FP8X4),
                            rhs_scale=w_scales[:],
                            start=True,
                            stop=True,
                        )
                    dl_banks[c, h, pair] = bank

        dl = {(c, pair): keep.tile([P, 2, CHUNK], F32, name=f"dl{c}_{pair}") for c in range(CHUNKS) for pair in range(2)}

        def empty_sums(c, h, pair, on_vector):
            dst = dl[c, pair][:, :, h * PART : (h + 1) * PART]
            if on_vector:
                nc.vector.tensor_copy(out=dst, in_=dl_banks[c, h, pair][:])
            else:
                nc.scalar.activation(dst, dl_banks[c, h, pair][:], COPY)

        def scatter(j, c, h0, h1, on_vector):
            src = dl[c, j // 2][:, j % 2, h0 * PART : h1 * PART]
            first_col = c * LIST_COLS
            dst = df[j][:].indirect(place_list[:, first_col + h0 * PART // 16 : first_col + h1 * PART // 16])
            if on_vector:
                nc.vector.tensor_copy(dst, src)
            else:
                nc.scalar.activation(dst, src, COPY)

        y = keep.tile([P, PACK, M], F32, name="y")
        out_rows = out_0.rearrange("(p j) m -> p j m", j=PACK)

        def add_old(j, cols):
            nc.vector.tensor_tensor(y[:, j, cols], old_sb[j][:, cols], df[j][:, cols], ALU.add)

        def store_rows(j):
            nc.sync.dma_start(out=out_rows[:, j, :], in_=y[:, j, :])

        y_codes = keep.tile([P, M], U32, name="y_codes", align_bytes=64)
        y_scales = keep.tile([P, M], U8, name="y_scales", align_bytes=64)
        y_bf = [keep.tile([P, QUARTER, PACK], BF16, name=f"y_bf{k}", align_bytes=64) for k in range(4)]

        def weave(k, on_vector):
            cols = slice(k * QUARTER, (k + 1) * QUARTER)
            dst = y_bf[k][:].rearrange("p (b i) j -> p b j i", i=4)
            src = y[:, :, cols].rearrange("p j (b i) -> p b j i", i=4)
            if on_vector:
                nc.vector.tensor_copy(out=dst, in_=src)
            else:
                nc.scalar.activation(dst, src, COPY)

        def quantise_y(k):
            cols = slice(k * QUARTER, (k + 1) * QUARTER)
            nc.vector.quantize_mx(
                out=y_codes[:, cols].bitcast(FP8X4), scales=y_scales[:, cols], in_=y_bf[k][:].rearrange("p m j -> p (m j)")
            )

        for r in range(PACK):
            empty_scores(r)
            for n in range(3):
                gather(n, r, 0)
            if r == 1:
                deal_msgs()
            if r > 0:
                weigh(r - 1, 0)
        quantise_msgs()
        weigh(PACK - 1, 0)
        for r in range(PACK):
            gather(1, r, 1)
            gather(2, r, 1)
        gather(0, 0, 1)
        multiply(0)
        for r in range(PACK):
            if r + 1 < PACK:
                gather(0, r + 1, 1)
            weigh(r, 1)
        for pair in range(2):
            empty_sums(0, 0, pair, False)
            empty_sums(0, 1, pair, False)
            scatter(2 * pair, 0, 0, 2, False)
            scatter(2 * pair + 1, 0, 0, 2, False)
        multiply(1)
        empty_sums(1, 0, 0, True)
        scatter(0, 1, 0, 1, True)
        empty_sums(1, 1, 0, True)
        scatter(0, 1, 1, 2, True)
        scatter(1, 1, 0, 1, True)
        scatter(1, 1, 1, 2, False)
        empty_sums(1, 0, 1, False)
        empty_sums(1, 1, 1, False)
        scatter(2, 1, 0, 2, False)
        scatter(3, 1, 0, 2, False)
        whole = slice(0, M)
        for j in range(3):
            add_old(j, whole)
            store_rows(j)
        for k in range(4):
            add_old(3, slice(k * QUARTER, (k + 1) * QUARTER))
        store_rows(3)
        weave(0, False)
        weave(1, True)
        weave(2, False)
        weave(3, True)
        words_out = out_1[0].rearrange("p m t -> p (m t)").bitcast(I32)
        for k in (1, 0, 3, 2):
            quantise_y(k)
            cols = slice(k * QUARTER, (k + 1) * QUARTER)
            nc.sync.dma_start(out=words_out[:, cols], in_=y_codes[:, cols].bitcast(I32))
        for quad in range(4):
            eng = nc.scalar if quad % 2 else nc.sync
            eng.dma_start(
                out=out_2[0, 4 * quad : 4 * quad + 4, :].bitcast(I32),
                in_=y_scales[32 * quad : 32 * quad + 4, :].bitcast(I32),
            )
